import numpy as np
import ml_dtypes


def mxq(x, axis, fmt="e4m3"):
    dtype, down = {"e4m3": (ml_dtypes.float8_e4m3fn, 7), "e5m2": (ml_dtypes.float8_e5m2, 14)}[fmt]
    v = np.moveaxis(np.asarray(x, np.float32).astype(ml_dtypes.bfloat16).astype(np.float64), axis, -1)
    blocks = v.reshape(v.shape[:-1] + (-1, 32))
    amax = np.abs(blocks).max(-1, keepdims=True)
    byte = np.maximum(np.where(amax > 0, np.frexp(amax)[1] - 1 + 127, 0) - down, 1)
    scale = np.exp2(byte - 127.0)
    codes = (blocks / scale).astype(np.float32).astype(dtype).astype(np.float64)
    return np.moveaxis((codes * scale).reshape(v.shape), -1, axis)


WIDE = False


def mx_kscale(k):
    if not WIDE:
        return np.ones(k)
    levels = np.array([10, -10, 5, -5, 0])
    if k % 512:
        return np.exp2(np.random.permutation(np.resize(levels, k // 32))).repeat(32)
    a = np.empty((k // 512, 16))
    for p in range(k // 512):
        a[p, :8] = np.random.permutation(np.resize(levels, 8))
        for g in range(8):
            far = levels[np.abs(levels - a[p, g]) >= 10]
            a[p, g + 8] = far[np.random.randint(len(far))]
    return np.exp2(a.ravel()).repeat(32)


BF16 = ml_dtypes.bfloat16


def bf(x):
    return np.asarray(x, np.float32).astype(BF16)


def f64(x):
    return np.asarray(x).astype(np.float64)


B, P, D, A, V = 1024, 512, 512, 512, 512


def draw0():
    s, t = mx_kscale(P), mx_kscale(D)
    return {
        "h_prev": bf(np.random.standard_normal((B, P)) * s),
        "q": bf(np.random.standard_normal((B, D)) * t),
        "wg": bf(np.random.standard_normal((P, D)) / np.sqrt(P) / s[:, None] * t),
        "bg": bf(np.random.standard_normal(D) * 0.3 * t),
        "wv": bf(np.random.standard_normal((D, V)) / np.sqrt(D) / t[:, None]),
        "wk": bf(np.random.standard_normal((D, A)) / np.sqrt(D) / t[:, None]),
        "wq": bf(np.random.standard_normal((D, A)) / np.sqrt(D) / t[:, None]),
    }


def _project(u, wv, wk, wq):
    value = u @ wv
    k = u @ wk
    r = u @ wq
    return value, k, r


def _score(k, r):
    return np.sum(k * r, axis=-1) / np.sqrt(A)


def core(h_prev, q, wg, bg, wv, wk, wq):
    p = (mxq(f64(h_prev), 1, "e4m3") @ mxq(f64(wg), 0, "e4m3")) + f64(bg)

    pm = mxq(p, 1, "e4m3")
    qm = mxq(f64(q), 1, "e4m3")
    wvm = mxq(f64(wv), 0, "e4m3")
    wkm = mxq(f64(wk), 0, "e4m3")
    wqm = mxq(f64(wq), 0, "e4m3")

    vp, kp, rp = _project(pm, wvm, wkm, wqm)
    vq, kq, rq = _project(qm, wvm, wkm, wqm)

    sp = _score(kp, rp)
    sq = _score(kq, rq)

    logits = np.stack([sp, sq], axis=-1)
    e = np.exp(logits - logits.max(axis=-1, keepdims=True))
    weights = e / e.sum(axis=-1, keepdims=True)
    ap = weights[:, 0]
    aq = weights[:, 1]

    z = ap[:, None] * vp + aq[:, None] * vq
    return z


def e4m3fn_bytes(y):
    return np.clip(np.asarray(y, np.float64), -448.0, 448.0).astype(np.float32).astype(ml_dtypes.float8_e4m3fn).view(np.uint8)


def e4m3fn_values(b):
    return np.asarray(b, np.uint8).view(ml_dtypes.float8_e4m3fn).astype(np.float64)


def setup_inputs():
    d = draw0()
    x0 = np.asarray(d['q']).astype(np.float64)
    s = (np.max(np.abs(x0), axis=(0,), keepdims=True) / 448.0).astype(np.float32)
    out = {}
    for k, v in d.items():
        if k == 'q':
            out['q_bytes'] = e4m3fn_bytes(x0 / s.astype(np.float64))
            out['q_scale'] = s
        else:
            out[k] = v
    return out


def reference(h_prev, q_bytes, q_scale, wg, bg, wv, wk, wq):
    return core(h_prev, e4m3fn_values(q_bytes) * q_scale.astype(np.float64), wg, bg, wv, wk, wq)

@@ -1,0 +1,350 @@
+import math
+from contextlib import ExitStack
+
+import concourse.mybir as mybir
+from concourse.masks import make_identity
+
+B, D = 1024, 512
+FLOPS = 7 * 2 * B * D * D
+
+F32 = mybir.dt.float32
+BF16 = mybir.dt.bfloat16
+U32 = mybir.dt.uint32
+U8 = mybir.dt.uint8
+FP8 = mybir.dt.float8_e4m3fn
+FP8X4 = mybir.dt.float8_e4m3fn_x4
+ALU = mybir.AluOpType
+ACT = mybir.ActivationFunctionType
+
+P = 128
+PACK = 4
+TILES = B // P
+PAIRS = TILES // 2
+RUN = 4
+WK_V = 128
+WQ_V = 128
+WG_V = 64
+WV_PIECES = 4
+Q_LEAD = 2
+
+
+def tile_aitmadaptiveinformationtransfer_kernel(tc, h_prev, q_bytes, q_scale, wg, bg, wv, wk, wq, out):
+    nc = tc.nc
+    half_inv_sqrt = 0.5 / math.sqrt(D)
+    h_rows = h_prev.rearrange("(p i) k -> p (i k)", i=TILES)
+    q_rows = q_bytes.rearrange("(p i) k -> p (i k)", i=TILES)
+    out_rows = out.rearrange("(p i) k -> p (i k)", i=TILES)
+
+    with ExitStack() as ctx:
+        keep = ctx.enter_context(tc.tile_pool(name="keep", bufs=1))
+        work = ctx.enter_context(tc.tile_pool(name="work", bufs=3))
+        psum = ctx.enter_context(tc.psum_pool(name="psum", bufs=1))
+        ctx.enter_context(tc.manual_schedule())
+
+        def kept(shape, dtype, name):
+            return keep.tile(shape, dtype, name=name, align_bytes=256)
+
+        def copy_on(engine, dst, src):
+            if engine == "vector":
+                nc.vector.tensor_copy(out=dst, in_=src)
+            else:
+                nc.scalar.activation(out=dst, in_=src, func=ACT.Copy)
+
+        raw = {}
+        grouped = {}
+
+        def load_weight(name, w):
+            raw[name] = kept([P, PACK * D], BF16, name + "_raw")
+            grouped[name] = kept([P, PACK * D], BF16, name + "_grouped")
+            nc.sync.dma_start(out=raw[name][:], in_=w.rearrange("(p j) c -> p (j c)", j=PACK))
+
+        h_sb = {}
+
+        def load_h(pair):
+            h_sb[pair] = kept([P, 2 * D], BF16, "h_sb%d" % pair)
+            nc.sync.dma_start(out=h_sb[pair][:], in_=h_rows[:, 2 * D * pair : 2 * D * (pair + 1)])
+
+        scale_cols = kept([P, PACK], F32, "scale_cols")
+        nc.sync.dma_start(out=scale_cols[:], in_=q_scale.rearrange("o (p t) -> p (o t)", t=PACK))
+        q_in = {}
+
+        def load_q(half):
+            q_in[half] = kept([P, PAIRS * D], U8, "q_bytes_sb%d" % half)
+            nc.sync.dma_start(out=q_in[half][:], in_=q_rows[:, PAIRS * D * half : PAIRS * D * (half + 1)])
+
+        bias_cols = kept([P, PACK], BF16, "bias_cols")
+        load_weight("wg", wg)
+        load_h(0)
+        load_q(0)
+        nc.sync.dma_start(out=bias_cols[:], in_=bg.rearrange("(p t) -> p t", t=PACK))
+        load_weight("wk", wk)
+        load_weight("wq", wq)
+        load_h(1)
+        load_q(1)
+        load_weight("wv", wv)
+        load_h(2)
+        load_h(3)
+
+        ident = kept([P, P], F32, "ident")
+        make_identity(nc, ident[:])
+
+        mx = {}
+
+        def quantize(name):
+            src = grouped[name][:]
+            width = src.shape[1] // PACK
+            codes = kept([P, width], U32, name + "_codes")
+            scales = kept([P, width], U8, name + "_scales")
+            nc.vector.quantize_mx(out=codes[:].bitcast(FP8X4), scales=scales[:], in_=src)
+            mx[name] = (codes, scales)
+
+        def matmul(dst, stationary, s_cols, moving, m_cols):
+            nc.tensor.matmul_mx(
+                out=dst,
+                lhsT=mx[stationary][0][:, s_cols].bitcast(FP8X4),
+                lhsT_scale=mx[stationary][1][:, s_cols],
+                rhs=mx[moving][0][:, m_cols].bitcast(FP8X4),
+                rhs_scale=mx[moving][1][:, m_cols],
+                start=True,
+                stop=True,
+            )
+
+        def interleave(name, engine, lo, hi):
+            dst = grouped[name][:, PACK * lo : PACK * hi].rearrange("p (c i j) -> p c j i", i=RUN, j=PACK)
+            src = raw[name][:].rearrange("p (j c) -> p j c", j=PACK)[:, :, lo:hi]
+            copy_on(engine, dst, src.rearrange("p j (c i) -> p c j i", i=RUN))
+
+        def interleave_wg(engine, lo, hi):
+            dst = grouped["wg"][:].rearrange("p (t m j) -> p m t j", t=PACK, j=PACK)[:, :, lo:hi]
+            src = raw["wg"][:].rearrange("p (j m t) -> p m t j", j=PACK, t=PACK)[:, :, lo:hi]
+            copy_on(engine, dst, src)
+
+        scale_bank = psum.tile([P, D], F32, name="scale_bank", tag="value_q")
+        for t in range(PACK):
+            nc.tensor.transpose(scale_bank[:, t::PACK], scale_cols[:, t : t + 1].to_broadcast([P, P]), ident[:])
+
+        q_sb = {}
+
+        def widen_q(i):
+            pair, half = divmod(i, 2)
+            if half == 0:
+                q_sb[pair] = kept([P, 2 * D], BF16, "q_sb%d" % pair)
+            nc.vector.tensor_tensor(
+                out=q_sb[pair][:, D * half : D * (half + 1)],
+                in0=q_in[i // PAIRS][:, D * (i % PAIRS) : D * (i % PAIRS + 1)].bitcast(FP8),
+                in1=scale_bank[:],
+                op=ALU.mult,
+            )
+
+        turn_bank = {}
+
+        def turn(name, rows, tag):
+            words = rows[:].bitcast(F32)
+            turn_bank[name] = psum.tile([P, D], F32, name="turn_bank", tag=tag)
+            for half in range(2):
+                for u in range(2):
+                    col = P * (2 * half + u)
+                    nc.tensor.transpose(
+                        turn_bank[name][:, col : col + P],
+                        words[:, 2 * P * half + u : 2 * P * (half + 1) : 2],
+                        ident[:],
+                    )
+
+        def empty_turn(name):
+            grouped[name] = kept([P, 2 * D], BF16, name + "_grouped")
+            nc.scalar.copy(
+                out=grouped[name][:].bitcast(F32).rearrange("p (i n u) -> p i n u", i=2, u=2),
+                in_=turn_bank[name][:].rearrange("p (i u n) -> p i n u", i=2, u=2),
+            )
+
+        def tokens(i):
+            return slice(P * (i % 2), P * (i % 2 + 1))
+
+        p_bank = {}
+
+        def project_p(i):
+            p_bank[i] = psum.tile([P, D], F32, name="p_bank", tag="p_bank")
+            for t in range(PACK):
+                cols = slice(P * t, P * (t + 1))
+                matmul(p_bank[i][:, cols], "wg", cols, "h%d" % (i // 2), tokens(i))
+
+        def add_bias(i):
+            name = "p%d" % i
+            grouped[name] = kept([P, D], BF16, name + "_grouped")
+            nc.vector.tensor_tensor(
+                out=grouped[name][:].rearrange("p (n t) -> p n t", t=PACK),
+                in0=p_bank[i][:].rearrange("p (t n) -> p n t", t=PACK),
+                in1=bias_cols[:].unsqueeze(1).to_broadcast([P, P, PACK]),
+                op=ALU.add,
+            )
+
+        def operand(side, i):
+            if side == "p":
+                return "p%d" % i, slice(0, P)
+            return "q%d" % (i // 2), tokens(i)
+
+        everything = slice(0, D)
+        key_sb = {}
+        query_bank = {}
+        score = {}
+
+        key_bank = {}
+
+        def project(side, i, weight, bank, role, tag=None):
+            name, cols = operand(side, i)
+            bank[side, i] = psum.tile([P, D], F32, name=role + "_bank", tag=tag or role + "_" + side)
+            matmul(bank[side, i][:], name, cols, weight, everything)
+
+        def copy_key(side, i):
+            key_sb[side, i] = work.tile([P, D], F32, name="key_sb", tag="key_sb_" + side)
+            nc.scalar.copy(out=key_sb[side, i][:], in_=key_bank[side, i][:])
+
+        def scores(side, i):
+            score[side, i] = kept([P, 1], F32, "score_%s%d" % (side, i))
+            nc.vector.scalar_tensor_tensor(
+                out=key_sb[side, i][:],
+                in0=query_bank[side, i][:],
+                scalar=half_inv_sqrt if side == "p" else -half_inv_sqrt,
+                in1=key_sb[side, i][:],
+                op0=ALU.mult,
+                op1=ALU.mult,
+                accum_out=score[side, i][:],
+            )
+
+        gate = {}
+        value_bank = {}
+        z_sb = {}
+
+        def gates(i):
+            gate[i] = kept([P, 3], F32, "gate%d" % i)
+            nc.scalar.activation(out=gate[i][:, 2:3], in_=score["p", i][:], func=ACT.Tanh, bias=score["q", i][:])
+
+        def gates2(i):
+            for col, sign in ((0, 0.5), (1, -0.5)):
+                nc.scalar.activation(
+                    out=gate[i][:, col : col + 1], in_=gate[i][:, 2:3], func=ACT.Identity, scale=sign, bias=0.5
+                )
+
+        def weigh_p(i, lo=0, hi=D):
+            if lo == 0:
+                z_sb[i] = work.tile([P, D], F32, name="z_sb", tag="z_sb")
+            nc.scalar.activation(
+                out=z_sb[i][:, lo:hi], in_=value_bank["p", i][:, lo:hi], func=ACT.Copy, scale=gate[i][:, 0:1]
+            )
+
+        def combine(i, lo=0, hi=D):
+            nc.vector.scalar_tensor_tensor(
+                out=z_sb[i][:, lo:hi],
+                in0=value_bank["q", i][:, lo:hi],
+                scalar=gate[i][:, 1:2],
+                in1=z_sb[i][:, lo:hi],
+                op0=ALU.mult,
+                op1=ALU.add,
+            )
+            nc.sync.dma_start(out=out_rows[:, D * i + lo : D * i + hi], in_=z_sb[i][:, lo:hi])
+
+        def keys(side, i):
+            project(side, i, "wk", key_bank, "key")
+            project(side, i, "wq", query_bank, "query")
+
+        def values(i, tags=(None, None)):
+            project("p", i, "wv", value_bank, "value", tags[0])
+            project("q", i, "wv", value_bank, "value", tags[1])
+
+        piece = D // WV_PIECES
+        interleave_wg("vector", 0, 3)
+        interleave_wg("scalar", 3, 4)
+        turn("h0", h_sb[0], "turn")
+        empty_turn("h0")
+        quantize("wg")
+        widen_q(0)
+        interleave("wk", "scalar", WK_V, D)
+        quantize("h0")
+        project_p(0)
+        widen_q(1)
+        turn("q0", q_sb[0], "turn")
+        if WK_V:
+            interleave("wk", "vector", 0, WK_V)
+        add_bias(0)
+        project_p(1)
+        empty_turn("q0")
+        interleave("wq", "scalar", WQ_V, D)
+        widen_q(2)
+        quantize("p0")
+        add_bias(1)
+        turn("h1", h_sb[1], "turn")
+        quantize("wk")
+        if WQ_V:
+            interleave("wq", "vector", 0, WQ_V)
+        widen_q(3)
+        turn("q1", q_sb[1], "value_p")
+        empty_turn("h1")
+        quantize("q0")
+        quantize("wq")
+        keys("p", 0)
+        keys("q", 0)
+        quantize("p1")
+        empty_turn("q1")
+        copy_key("p", 0)
+        copy_key("q", 0)
+        quantize("h1")
+        project_p(2)
+        widen_q(4)
+        widen_q(5)
+        turn("h2", h_sb[2], "turn")
+        turn("q2", q_sb[2], "value_p")
+        interleave("wv", "scalar", 0, piece)
+        interleave("wv", "scalar", piece, 2 * piece)
+
+        late = {0: ("q1",), 1: ("h2", "wv"), 2: ("q2", "h3"), 3: ("q3",)}
+        for s in range(TILES + 1):
+            if s < TILES:
+                scores("p", s)
+            if s + 2 < TILES:
+                add_bias(s + 2)
+            if s + 1 < TILES:
+                keys("p", s + 1)
+                copy_key("p", s + 1)
+            if s == 0:
+                empty_turn("h2")
+                empty_turn("q2")
+                quantize("q1")
+                widen_q(6)
+            if s == TILES - 1:
+                values(s, ("key_p", "key_q"))
+                weigh_p(s - 1)
+            if s < TILES:
+                scores("q", s)
+                gates(s)
+            if s + 1 < TILES:
+                keys("q", s + 1)
+                copy_key("q", s + 1)
+            if s + 2 < TILES:
+                quantize("p%d" % (s + 2))
+            if s == 0:
+                project_p(3)
+                widen_q(7)
+                turn("h3", h_sb[3], "turn")
+                turn("q3", q_sb[3], "value_p")
+                for k in (2, 3):
+                    interleave("wv", "scalar", piece * k, piece * (k + 1))
+            if s == 1:
+                empty_turn("h3")
+                empty_turn("q3")
+            for name in late.get(s, ()) if s else ():
+                quantize(name)
+            if 0 < s and s + 3 < TILES:
+                project_p(s + 3)
+            if s < TILES:
+                gates2(s)
+            if 2 <= s:
+                combine(s - 2)
+            if 1 <= s < TILES - 1:
+                values(s - 1)
+                weigh_p(s - 1)
+            if s == TILES - 2:
+                values(s, ("turn", "p_bank"))
+        for lo in (0, D // 2):
+            weigh_p(TILES - 1, lo, lo + D // 2)
+        for lo in (0, D // 2):
+            combine(TILES - 1, lo, lo + D // 2)

@@ -21,11 +21,12 @@ PACK = 4
 TILES = B // P
 PAIRS = TILES // 2
 RUN = 4
-WK_V = 128
-WQ_V = 128
-WG_V = 64
+WK_V = 384
+WQ_V = 0
+WG_V = 2
 WV_PIECES = 4
-Q_LEAD = 2
+LAG = 2
+ASIDE = (0, 1, 2, 3)
 
 
 def tile_aitmadaptiveinformationtransfer_kernel(tc, h_prev, q_bytes, q_scale, wg, bg, wv, wk, wq, out):
@@ -37,7 +38,7 @@ def tile_aitmadaptiveinformationtransfer_kernel(tc, h_prev, q_bytes, q_scale, wg
 
     with ExitStack() as ctx:
         keep = ctx.enter_context(tc.tile_pool(name="keep", bufs=1))
-        work = ctx.enter_context(tc.tile_pool(name="work", bufs=3))
+        work = ctx.enter_context(tc.tile_pool(name="work", bufs=5))
         psum = ctx.enter_context(tc.psum_pool(name="psum", bufs=1))
         ctx.enter_context(tc.manual_schedule())
 
@@ -47,8 +48,10 @@ def tile_aitmadaptiveinformationtransfer_kernel(tc, h_prev, q_bytes, q_scale, wg
         def copy_on(engine, dst, src):
             if engine == "vector":
                 nc.vector.tensor_copy(out=dst, in_=src)
-            else:
+            elif engine == "scalar":
                 nc.scalar.activation(out=dst, in_=src, func=ACT.Copy)
+            else:
+                nc.gpsimd.tensor_scalar(out=dst, in0=src, scalar1=1.0, scalar2=0.0, op0=ALU.mult, op1=ALU.add)
 
         raw = {}
         grouped = {}
@@ -73,14 +76,14 @@ def tile_aitmadaptiveinformationtransfer_kernel(tc, h_prev, q_bytes, q_scale, wg
             nc.sync.dma_start(out=q_in[half][:], in_=q_rows[:, PAIRS * D * half : PAIRS * D * (half + 1)])
 
         bias_cols = kept([P, PACK], BF16, "bias_cols")
-        load_weight("wg", wg)
-        load_h(0)
         load_q(0)
-        nc.sync.dma_start(out=bias_cols[:], in_=bg.rearrange("(p t) -> p t", t=PACK))
+        load_weight("wg", wg)
         load_weight("wk", wk)
+        load_q(1)
+        load_h(0)
+        nc.sync.dma_start(out=bias_cols[:], in_=bg.rearrange("(p t) -> p t", t=PACK))
         load_weight("wq", wq)
         load_h(1)
-        load_q(1)
         load_weight("wv", wv)
         load_h(2)
         load_h(3)
@@ -172,9 +175,9 @@ def tile_aitmadaptiveinformationtransfer_kernel(tc, h_prev, q_bytes, q_scale, wg
             name = "p%d" % i
             grouped[name] = kept([P, D], BF16, name + "_grouped")
             nc.vector.tensor_tensor(
-                out=grouped[name][:].rearrange("p (n t) -> p n t", t=PACK),
-                in0=p_bank[i][:].rearrange("p (t n) -> p n t", t=PACK),
-                in1=bias_cols[:].unsqueeze(1).to_broadcast([P, P, PACK]),
+                out=grouped[name][:].rearrange("p (n i t) -> p n t i", i=2, t=PACK),
+                in0=p_bank[i][:].rearrange("p (t n i) -> p n t i", i=2, t=PACK),
+                in1=bias_cols[:].unsqueeze(1).unsqueeze(3).to_broadcast([P, P // 2, PACK, 2]),
                 op=ALU.add,
             )
 
@@ -243,107 +246,128 @@ def tile_aitmadaptiveinformationtransfer_kernel(tc, h_prev, q_bytes, q_scale, wg
             )
             nc.sync.dma_start(out=out_rows[:, D * i + lo : D * i + hi], in_=z_sb[i][:, lo:hi])
 
-        def keys(side, i):
-            project(side, i, "wk", key_bank, "key")
-            project(side, i, "wq", query_bank, "query")
+        def combine_aside(i):
+            zq_sb = work.tile([P, D], F32, name="zq_sb", tag="zq_sb")
+            nc.scalar.activation(out=zq_sb[:], in_=value_bank["q", i][:], func=ACT.Copy, scale=gate[i][:, 1:2])
+            nc.gpsimd.tensor_tensor(out=z_sb[i][:], in0=z_sb[i][:], in1=zq_sb[:], op=ALU.add)
+            nc.sync.dma_start(out=out_rows[:, D * i : D * (i + 1)], in_=z_sb[i][:])
+
+        def keys(side, i, tags=(None, None)):
+            project(side, i, "wk", key_bank, "key", tags[0])
+            project(side, i, "wq", query_bank, "query", tags[1])
 
         def values(i, tags=(None, None)):
             project("p", i, "wv", value_bank, "value", tags[0])
             project("q", i, "wv", value_bank, "value", tags[1])
 
         piece = D // WV_PIECES
-        interleave_wg("vector", 0, 3)
-        interleave_wg("scalar", 3, 4)
-        turn("h0", h_sb[0], "turn")
-        empty_turn("h0")
-        quantize("wg")
+        interleave_wg("gpsimd", 0, WG_V)
+        interleave_wg("scalar", WG_V, 4)
+        interleave("wk", "gpsimd", 0, WK_V)
         widen_q(0)
-        interleave("wk", "scalar", WK_V, D)
-        quantize("h0")
-        project_p(0)
         widen_q(1)
         turn("q0", q_sb[0], "turn")
-        if WK_V:
-            interleave("wk", "vector", 0, WK_V)
-        add_bias(0)
-        project_p(1)
         empty_turn("q0")
-        interleave("wq", "scalar", WQ_V, D)
+        if WK_V < D:
+            interleave("wk", "scalar", WK_V, D)
         widen_q(2)
-        quantize("p0")
-        add_bias(1)
-        turn("h1", h_sb[1], "turn")
+        widen_q(3)
+        turn("h0", h_sb[0], "key_p")
+        empty_turn("h0")
+        turn("q1", q_sb[1], "turn")
+        interleave("wq", "scalar", WQ_V, D)
+        for i in range(4, TILES):
+            widen_q(i)
+        turn("h1", h_sb[1], "key_p")
+        turn("q2", q_sb[2], "value_p")
+        quantize("wg")
+        quantize("h0")
+        project_p(0)
+        turn("q3", q_sb[3], "value_q")
         quantize("wk")
+        quantize("q0")
+        empty_turn("h1")
+        empty_turn("q1")
         if WQ_V:
             interleave("wq", "vector", 0, WQ_V)
-        widen_q(3)
-        turn("q1", q_sb[1], "value_p")
-        empty_turn("h1")
-        quantize("q0")
+        add_bias(0)
+        project_p(1)
+        empty_turn("q2")
+        empty_turn("q3")
         quantize("wq")
-        keys("p", 0)
         keys("q", 0)
-        quantize("p1")
-        empty_turn("q1")
-        copy_key("p", 0)
+        quantize("p0")
+        keys("p", 0)
+        turn("h2", h_sb[2], "turn")
+        turn("h3", h_sb[3], "value_p")
+        add_bias(1)
         copy_key("q", 0)
+        copy_key("p", 0)
+        interleave("wv", "scalar", 0, piece)
         quantize("h1")
         project_p(2)
-        widen_q(4)
-        widen_q(5)
-        turn("h2", h_sb[2], "turn")
-        turn("q2", q_sb[2], "value_p")
-        interleave("wv", "scalar", 0, piece)
-        interleave("wv", "scalar", piece, 2 * piece)
+        quantize("q1")
+        quantize("p1")
+        quantize("q2")
+        quantize("q3")
+        scores("q", 0)
+        keys("q", 1)
+        copy_key("q", 1)
 
-        late = {0: ("q1",), 1: ("h2", "wv"), 2: ("q2", "h3"), 3: ("q3",)}
-        for s in range(TILES + 1):
-            if s < TILES:
-                scores("p", s)
-            if s + 2 < TILES:
-                add_bias(s + 2)
-            if s + 1 < TILES:
-                keys("p", s + 1)
-                copy_key("p", s + 1)
+        late = {1: ("wv", "h2", "h3")}
+        last = TILES - 1
+        for s in range(TILES - 2):
+            scores("p", s)
+            gates(s)
+            add_bias(s + 2)
+            keys("p", s + 1)
             if s == 0:
+                interleave("wv", "scalar", piece, 2 * piece)
+            copy_key("p", s + 1)
+            gates2(s)
+            scores("q", s + 1)
+            keys("q", s + 2)
+            copy_key("q", s + 2)
+            if s == 0:
+                interleave("wv", "scalar", 2 * piece, 3 * piece)
                 empty_turn("h2")
-                empty_turn("q2")
-                quantize("q1")
-                widen_q(6)
-            if s == TILES - 1:
-                values(s, ("key_p", "key_q"))
-                weigh_p(s - 1)
-            if s < TILES:
-                scores("q", s)
-                gates(s)
-            if s + 1 < TILES:
-                keys("q", s + 1)
-                copy_key("q", s + 1)
-            if s + 2 < TILES:
-                quantize("p%d" % (s + 2))
-            if s == 0:
-                project_p(3)
-                widen_q(7)
-                turn("h3", h_sb[3], "turn")
-                turn("q3", q_sb[3], "value_p")
-                for k in (2, 3):
-                    interleave("wv", "scalar", piece * k, piece * (k + 1))
+                interleave("wv", "scalar", 3 * piece, 4 * piece)
             if s == 1:
                 empty_turn("h3")
-                empty_turn("q3")
-            for name in late.get(s, ()) if s else ():
-                quantize(name)
-            if 0 < s and s + 3 < TILES:
+                quantize("h2")
+            quantize("p%d" % (s + 2))
+            if s == 1:
+                quantize("wv")
+            if s == 2:
+                quantize("h3")
+            if s + 3 < TILES:
                 project_p(s + 3)
-            if s < TILES:
-                gates2(s)
+            else:
+                keys("p", last, ("turn", "p_bank"))
+                copy_key("p", last)
+            if s == 1:
+                project("p", 0, "wv", value_bank, "value", "turn")
+                weigh_p(0)
             if 2 <= s:
                 combine(s - 2)
-            if 1 <= s < TILES - 1:
-                values(s - 1)
-                weigh_p(s - 1)
-            if s == TILES - 2:
-                values(s, ("turn", "p_bank"))
+            if 1 <= s:
+                project("p", s, "wv", value_bank, "value")
+                project("q", s - 1, "wv", value_bank, "value")
+                weigh_p(s)
+        scores("p", last - 1)
+        gates(last - 1)
+        project("p", last - 1, "wv", value_bank, "value", "key_p")
+        project("q", last - 2, "wv", value_bank, "value", "key_q")
+        project("q", last - 1, "wv", value_bank, "value", "query_p")
+        values(last, ("turn", "value_p"))
+        gates2(last - 1)
+        scores("q", last)
+        weigh_p(last - 1)
+        scores("p", last)
+        gates(last)
+        gates2(last)
+        for i in range(last - 3, last):
+            combine(i)
         for lo in (0, D // 2):
             weigh_p(TILES - 1, lo, lo + D // 2)
         for lo in (0, D // 2):

@@ -21,12 +21,13 @@ PACK = 4
 TILES = B // P
 PAIRS = TILES // 2
 RUN = 4
-WK_V = 384
+WK_V = 320
 WQ_V = 0
 WG_V = 2
 WV_PIECES = 4
-LAG = 2
-ASIDE = (0, 1, 2, 3)
+KEY_EARLY = 6
+LAG = 3
+ASIDE = (1, 3)
 
 
 def tile_aitmadaptiveinformationtransfer_kernel(tc, h_prev, q_bytes, q_scale, wg, bg, wv, wk, wq, out):
@@ -58,7 +59,6 @@ def tile_aitmadaptiveinformationtransfer_kernel(tc, h_prev, q_bytes, q_scale, wg
 
         def load_weight(name, w):
             raw[name] = kept([P, PACK * D], BF16, name + "_raw")
-            grouped[name] = kept([P, PACK * D], BF16, name + "_grouped")
             nc.sync.dma_start(out=raw[name][:], in_=w.rearrange("(p j) c -> p (j c)", j=PACK))
 
         h_sb = {}
@@ -82,24 +82,27 @@ def tile_aitmadaptiveinformationtransfer_kernel(tc, h_prev, q_bytes, q_scale, wg
         load_q(1)
         load_h(0)
         nc.sync.dma_start(out=bias_cols[:], in_=bg.rearrange("(p t) -> p t", t=PACK))
-        load_weight("wq", wq)
         load_h(1)
-        load_weight("wv", wv)
         load_h(2)
         load_h(3)
+        load_weight("wq", wq)
+        load_weight("wv", wv)
 
         ident = kept([P, P], F32, "ident")
         make_identity(nc, ident[:])
 
         mx = {}
 
-        def quantize(name):
-            src = grouped[name][:]
+        def quantize(name, lo=0, hi=None):
+            src = grouped[name]
             width = src.shape[1] // PACK
-            codes = kept([P, width], U32, name + "_codes")
-            scales = kept([P, width], U8, name + "_scales")
-            nc.vector.quantize_mx(out=codes[:].bitcast(FP8X4), scales=scales[:], in_=src)
-            mx[name] = (codes, scales)
+            if name not in mx:
+                mx[name] = (kept([P, width], U32, name + "_codes"), kept([P, width], U8, name + "_scales"))
+            hi = width if hi is None else hi
+            codes, scales = mx[name]
+            nc.vector.quantize_mx(
+                out=codes[:, lo:hi].bitcast(FP8X4), scales=scales[:, lo:hi], in_=src[:, PACK * lo : PACK * hi]
+            )
 
         def matmul(dst, stationary, s_cols, moving, m_cols):
             nc.tensor.matmul_mx(
@@ -112,6 +115,9 @@ def tile_aitmadaptiveinformationtransfer_kernel(tc, h_prev, q_bytes, q_scale, wg
                 stop=True,
             )
 
+        def w_grouped(name, slot):
+            grouped[name] = keep.tile([P, PACK * D], BF16, name=name + "_grouped", tag=slot, align_bytes=256)
+
         def interleave(name, engine, lo, hi):
             dst = grouped[name][:, PACK * lo : PACK * hi].rearrange("p (c i j) -> p c j i", i=RUN, j=PACK)
             src = raw[name][:].rearrange("p (j c) -> p j c", j=PACK)[:, :, lo:hi]
@@ -122,7 +128,7 @@ def tile_aitmadaptiveinformationtransfer_kernel(tc, h_prev, q_bytes, q_scale, wg
             src = raw["wg"][:].rearrange("p (j m t) -> p m t j", j=PACK, t=PACK)[:, :, lo:hi]
             copy_on(engine, dst, src)
 
-        scale_bank = psum.tile([P, D], F32, name="scale_bank", tag="value_q")
+        scale_bank = psum.tile([P, D], F32, name="scale_bank", tag="b7")
         for t in range(PACK):
             nc.tensor.transpose(scale_bank[:, t::PACK], scale_cols[:, t : t + 1].to_broadcast([P, P]), ident[:])
 
@@ -139,52 +145,47 @@ def tile_aitmadaptiveinformationtransfer_kernel(tc, h_prev, q_bytes, q_scale, wg
                 op=ALU.mult,
             )
 
+        for side in ("h", "q", "p"):
+            grouped[side] = keep.tile([P, PACK * B], BF16, name=side + "_grouped", tag="slot_" + side, align_bytes=256)
         turn_bank = {}
 
-        def turn(name, rows, tag):
-            words = rows[:].bitcast(F32)
-            turn_bank[name] = psum.tile([P, D], F32, name="turn_bank", tag=tag)
+        def turn(side, pair, tag):
+            words = (h_sb if side == "h" else q_sb)[pair][:].bitcast(F32)
+            turn_bank[side, pair] = psum.tile([P, D], F32, name="turn_bank", tag=tag)
             for half in range(2):
                 for u in range(2):
                     col = P * (2 * half + u)
                     nc.tensor.transpose(
-                        turn_bank[name][:, col : col + P],
+                        turn_bank[side, pair][:, col : col + P],
                         words[:, 2 * P * half + u : 2 * P * (half + 1) : 2],
                         ident[:],
                     )
 
-        def empty_turn(name):
-            grouped[name] = kept([P, 2 * D], BF16, name + "_grouped")
+        def empty_turn(side, pair):
+            dst = grouped[side][:, 2 * D * pair : 2 * D * (pair + 1)].bitcast(F32)
             nc.scalar.copy(
-                out=grouped[name][:].bitcast(F32).rearrange("p (i n u) -> p i n u", i=2, u=2),
-                in_=turn_bank[name][:].rearrange("p (i u n) -> p i n u", i=2, u=2),
+                out=dst.rearrange("p (i n u) -> p i n u", i=2, u=2),
+                in_=turn_bank[side, pair][:].rearrange("p (i u n) -> p i n u", i=2, u=2),
             )
 
         def tokens(i):
-            return slice(P * (i % 2), P * (i % 2 + 1))
+            return slice(P * i, P * (i + 1))
 
         p_bank = {}
 
-        def project_p(i):
-            p_bank[i] = psum.tile([P, D], F32, name="p_bank", tag="p_bank")
+        def project_p(i, tag):
+            p_bank[i] = psum.tile([P, D], F32, name="p_bank", tag=tag)
             for t in range(PACK):
                 cols = slice(P * t, P * (t + 1))
-                matmul(p_bank[i][:, cols], "wg", cols, "h%d" % (i // 2), tokens(i))
+                matmul(p_bank[i][:, cols], "wg", cols, "h", tokens(i))
 
         def add_bias(i):
-            name = "p%d" % i
-            grouped[name] = kept([P, D], BF16, name + "_grouped")
             nc.vector.tensor_tensor(
-                out=grouped[name][:].rearrange("p (n i t) -> p n t i", i=2, t=PACK),
+                out=grouped["p"][:, D * i : D * (i + 1)].rearrange("p (n i t) -> p n t i", i=2, t=PACK),
                 in0=p_bank[i][:].rearrange("p (t n i) -> p n t i", i=2, t=PACK),
                 in1=bias_cols[:].unsqueeze(1).unsqueeze(3).to_broadcast([P, P // 2, PACK, 2]),
                 op=ALU.add,
             )
-
-        def operand(side, i):
-            if side == "p":
-                return "p%d" % i, slice(0, P)
-            return "q%d" % (i // 2), tokens(i)
 
         everything = slice(0, D)
         key_sb = {}
@@ -193,13 +194,12 @@ def tile_aitmadaptiveinformationtransfer_kernel(tc, h_prev, q_bytes, q_scale, wg
 
         key_bank = {}
 
-        def project(side, i, weight, bank, role, tag=None):
-            name, cols = operand(side, i)
-            bank[side, i] = psum.tile([P, D], F32, name=role + "_bank", tag=tag or role + "_" + side)
-            matmul(bank[side, i][:], name, cols, weight, everything)
+        def project(side, i, weight, bank, tag):
+            bank[side, i] = psum.tile([P, D], F32, name="result_bank", tag=tag)
+            matmul(bank[side, i][:], side, tokens(i), weight, everything)
 
         def copy_key(side, i):
-            key_sb[side, i] = work.tile([P, D], F32, name="key_sb", tag="key_sb_" + side)
+            key_sb[side, i] = kept([P, D], F32, "key_%s%d" % (side, i))
             nc.scalar.copy(out=key_sb[side, i][:], in_=key_bank[side, i][:])
 
         def scores(side, i):
@@ -250,124 +250,129 @@ def tile_aitmadaptiveinformationtransfer_kernel(tc, h_prev, q_bytes, q_scale, wg
             zq_sb = work.tile([P, D], F32, name="zq_sb", tag="zq_sb")
             nc.scalar.activation(out=zq_sb[:], in_=value_bank["q", i][:], func=ACT.Copy, scale=gate[i][:, 1:2])
             nc.gpsimd.tensor_tensor(out=z_sb[i][:], in0=z_sb[i][:], in1=zq_sb[:], op=ALU.add)
+
+        def store(i):
             nc.sync.dma_start(out=out_rows[:, D * i : D * (i + 1)], in_=z_sb[i][:])
 
-        def keys(side, i, tags=(None, None)):
-            project(side, i, "wk", key_bank, "key", tags[0])
-            project(side, i, "wq", query_bank, "query", tags[1])
-
-        def values(i, tags=(None, None)):
-            project("p", i, "wv", value_bank, "value", tags[0])
-            project("q", i, "wv", value_bank, "value", tags[1])
-
-        piece = D // WV_PIECES
+        w_grouped("wg", "slot_a")
+        w_grouped("wk", "slot_b")
+        w_grouped("wq", "slot_c")
         interleave_wg("gpsimd", 0, WG_V)
         interleave_wg("scalar", WG_V, 4)
         interleave("wk", "gpsimd", 0, WK_V)
         widen_q(0)
         widen_q(1)
-        turn("q0", q_sb[0], "turn")
-        empty_turn("q0")
+        turn("q", 0, "b0")
+        empty_turn("q", 0)
         if WK_V < D:
             interleave("wk", "scalar", WK_V, D)
         widen_q(2)
         widen_q(3)
-        turn("h0", h_sb[0], "key_p")
-        empty_turn("h0")
-        turn("q1", q_sb[1], "turn")
-        interleave("wq", "scalar", WQ_V, D)
+        turn("q", 1, "b1")
+        turn("h", 0, "b2")
+        turn("h", 1, "b3")
+        empty_turn("h", 0)
+        empty_turn("h", 1)
+        empty_turn("q", 1)
         for i in range(4, TILES):
             widen_q(i)
-        turn("h1", h_sb[1], "key_p")
-        turn("q2", q_sb[2], "value_p")
-        quantize("wg")
-        quantize("h0")
-        project_p(0)
-        turn("q3", q_sb[3], "value_q")
-        quantize("wk")
-        quantize("q0")
-        empty_turn("h1")
-        empty_turn("q1")
-        if WQ_V:
-            interleave("wq", "vector", 0, WQ_V)
-        add_bias(0)
-        project_p(1)
-        empty_turn("q2")
-        empty_turn("q3")
-        quantize("wq")
-        keys("q", 0)
-        quantize("p0")
-        keys("p", 0)
-        turn("h2", h_sb[2], "turn")
-        turn("h3", h_sb[3], "value_p")
-        add_bias(1)
-        copy_key("q", 0)
-        copy_key("p", 0)
-        interleave("wv", "scalar", 0, piece)
-        quantize("h1")
-        project_p(2)
-        quantize("q1")
-        quantize("p1")
-        quantize("q2")
-        quantize("q3")
-        scores("q", 0)
-        keys("q", 1)
-        copy_key("q", 1)
-
-        late = {1: ("wv", "h2", "h3")}
+        turn("q", 2, "b0")
+        turn("h", 2, "b4")
+        turn("h", 3, "b5")
+        turn("q", 3, "b2")
+        empty_turn("h", 2)
+        empty_turn("h", 3)
+        empty_turn("q", 2)
+        empty_turn("q", 3)
+        half = B // 2
         last = TILES - 1
-        for s in range(TILES - 2):
-            scores("p", s)
-            gates(s)
-            add_bias(s + 2)
-            keys("p", s + 1)
-            if s == 0:
-                interleave("wv", "scalar", piece, 2 * piece)
-            copy_key("p", s + 1)
-            gates2(s)
-            scores("q", s + 1)
-            keys("q", s + 2)
-            copy_key("q", s + 2)
-            if s == 0:
-                interleave("wv", "scalar", 2 * piece, 3 * piece)
-                empty_turn("h2")
-                interleave("wv", "scalar", 3 * piece, 4 * piece)
-            if s == 1:
-                empty_turn("h3")
-                quantize("h2")
-            quantize("p%d" % (s + 2))
+        p_tags = ("b6", "b7", "b3", "b4", "b5")
+        key_tags = ("b0", "b1", "b2")
+        v_tags = ("b3", "b0", "b1")
+
+        def key(side, i, tag):
+            project(side, i, "wk", key_bank, tag)
+            copy_key(side, i)
+
+        def queries(i):
+            project("q", i, "wq", query_bank, ("b4", "b6")[i % 2])
+            project("p", i, "wq", query_bank, ("b5", "b7")[i % 2])
+
+        interleave("wq", "scalar", 0, D)
+        quantize("wg")
+        quantize("h", 0, half)
+        for i in range(4):
+            project_p(i, p_tags[i])
+        quantize("wk")
+        quantize("q", 0, half)
+        add_bias(0)
+        quantize("h", half, B)
+        add_bias(1)
+        for i in range(4, 7):
+            project_p(i, p_tags[i % 5])
+        for i in range(3):
+            key("q", i, key_tags[i])
+        quantize("q", half, B)
+        add_bias(2)
+        project_p(7, p_tags[2])
+        key("q", 3, key_tags[0])
+        add_bias(3)
+        add_bias(4)
+        quantize("p", 0, half)
+        quantize("wq")
+        w_grouped("wv", "slot_c")
+        interleave("wv", "gpsimd", 0, D)
+        for i in range(5, TILES):
+            add_bias(i)
+        early = [("p", 0), ("q", 4), ("p", 1), ("q", 5), ("p", 2), ("q", 6), ("p", 3), ("q", 7)]
+        for n, (side, i) in enumerate(early):
+            key(side, i, key_tags[(n + 1) % 3])
+            if n in (1, 3):
+                queries(n // 2)
+            if n == 5:
+                scores("q", 0)
+                scores("p", 0)
+                queries(2)
+                gates(0)
+        gates2(0)
+
+        value_tags = {last - 1: ("b2", v_tags[1]), last: ("b4", "b5")}
+
+        def values(i):
+            tags = value_tags.get(i, (v_tags[(2 * i) % 3], v_tags[(2 * i + 1) % 3]))
+            project("p", i, "wv", value_bank, tags[0])
+            return tags[1]
+
+        for s in range(1, TILES + 1):
+            if s < TILES:
+                scores("q", s)
+                scores("p", s)
+            if s + 2 < TILES:
+                queries(s + 2)
             if s == 1:
                 quantize("wv")
-            if s == 2:
-                quantize("h3")
-            if s + 3 < TILES:
-                project_p(s + 3)
-            else:
-                keys("p", last, ("turn", "p_bank"))
-                copy_key("p", last)
-            if s == 1:
-                project("p", 0, "wv", value_bank, "value", "turn")
-                weigh_p(0)
-            if 2 <= s:
+                quantize("p", half, B)
+                project("q", 0, "wv", value_bank, values(0))
+            if s == last:
+                weigh_p(s - 1)
+            if s < TILES:
+                gates(s)
+            if s < last:
+                weigh_p(s - 1)
+            if s < TILES:
+                gates2(s)
+            if s - 1 in ASIDE:
+                combine_aside(s - 1)
+            if 2 <= s and s - 2 not in ASIDE:
                 combine(s - 2)
-            if 1 <= s:
-                project("p", s, "wv", value_bank, "value")
-                project("q", s - 1, "wv", value_bank, "value")
-                weigh_p(s)
-        scores("p", last - 1)
-        gates(last - 1)
-        project("p", last - 1, "wv", value_bank, "value", "key_p")
-        project("q", last - 2, "wv", value_bank, "value", "key_q")
-        project("q", last - 1, "wv", value_bank, "value", "query_p")
-        values(last, ("turn", "value_p"))
-        gates2(last - 1)
-        scores("q", last)
-        weigh_p(last - 1)
-        scores("p", last)
-        gates(last)
-        gates2(last)
-        for i in range(last - 3, last):
-            combine(i)
+            if s - 2 in ASIDE:
+                store(s - 2)
+            if s < TILES:
+                tag = values(s)
+            if s + 3 < TILES:
+                key("p", s + 3, "b2")
+            if s < TILES:
+                project("q", s, "wv", value_bank, tag)
         for lo in (0, D // 2):
             weigh_p(TILES - 1, lo, lo + D // 2)
         for lo in (0, D // 2):

@@ -20,88 +20,79 @@ P = 128
 PACK = 4
 TILES = B // P
 PAIRS = TILES // 2
+HALF = TILES // 2
+LAST = TILES - 1
 RUN = 4
-WK_V = 320
-WQ_V = 0
-WG_V = 2
-WV_PIECES = 4
-KEY_EARLY = 6
-LAG = 3
-ASIDE = (1, 3)
+
+GPSIMD_COLUMNS = {"wk": 256, "wq": 320, "wv": 384}
+ASIDE = (1, 2, 3)
+Z_BUFS = 5
 
 
 def tile_aitmadaptiveinformationtransfer_kernel(tc, h_prev, q_bytes, q_scale, wg, bg, wv, wk, wq, out):
     nc = tc.nc
-    half_inv_sqrt = 0.5 / math.sqrt(D)
     h_rows = h_prev.rearrange("(p i) k -> p (i k)", i=TILES)
     q_rows = q_bytes.rearrange("(p i) k -> p (i k)", i=TILES)
     out_rows = out.rearrange("(p i) k -> p (i k)", i=TILES)
 
     with ExitStack() as ctx:
         keep = ctx.enter_context(tc.tile_pool(name="keep", bufs=1))
-        work = ctx.enter_context(tc.tile_pool(name="work", bufs=5))
+        work = ctx.enter_context(tc.tile_pool(name="work", bufs=Z_BUFS))
         psum = ctx.enter_context(tc.psum_pool(name="psum", bufs=1))
         ctx.enter_context(tc.manual_schedule())
 
         def kept(shape, dtype, name):
             return keep.tile(shape, dtype, name=name, align_bytes=256)
 
-        def copy_on(engine, dst, src):
-            if engine == "vector":
-                nc.vector.tensor_copy(out=dst, in_=src)
-            elif engine == "scalar":
-                nc.scalar.activation(out=dst, in_=src, func=ACT.Copy)
-            else:
-                nc.gpsimd.tensor_scalar(out=dst, in0=src, scalar1=1.0, scalar2=0.0, op0=ALU.mult, op1=ALU.add)
+        def bank_tile(bank):
+            return psum.tile([P, D], F32, name="bank", tag="bank%d" % bank)
 
         raw = {}
-        grouped = {}
+        rows = {}
+        q_in = {}
 
         def load_weight(name, w):
             raw[name] = kept([P, PACK * D], BF16, name + "_raw")
             nc.sync.dma_start(out=raw[name][:], in_=w.rearrange("(p j) c -> p (j c)", j=PACK))
 
-        h_sb = {}
-
         def load_h(pair):
-            h_sb[pair] = kept([P, 2 * D], BF16, "h_sb%d" % pair)
-            nc.sync.dma_start(out=h_sb[pair][:], in_=h_rows[:, 2 * D * pair : 2 * D * (pair + 1)])
+            rows["h", pair] = kept([P, 2 * D], BF16, "h_rows%d" % pair)
+            nc.sync.dma_start(out=rows["h", pair][:], in_=h_rows[:, 2 * D * pair : 2 * D * (pair + 1)])
+
+        def load_q(half):
+            q_in[half] = kept([P, HALF * D], U8, "q_bytes_sb%d" % half)
+            nc.sync.dma_start(out=q_in[half][:], in_=q_rows[:, HALF * D * half : HALF * D * (half + 1)])
 
         scale_cols = kept([P, PACK], F32, "scale_cols")
         nc.sync.dma_start(out=scale_cols[:], in_=q_scale.rearrange("o (p t) -> p (o t)", t=PACK))
-        q_in = {}
-
-        def load_q(half):
-            q_in[half] = kept([P, PAIRS * D], U8, "q_bytes_sb%d" % half)
-            nc.sync.dma_start(out=q_in[half][:], in_=q_rows[:, PAIRS * D * half : PAIRS * D * (half + 1)])
-
-        bias_cols = kept([P, PACK], BF16, "bias_cols")
         load_q(0)
         load_weight("wg", wg)
         load_weight("wk", wk)
         load_q(1)
         load_h(0)
+        bias_cols = kept([P, PACK], BF16, "bias_cols")
         nc.sync.dma_start(out=bias_cols[:], in_=bg.rearrange("(p t) -> p t", t=PACK))
-        load_h(1)
-        load_h(2)
-        load_h(3)
+        for pair in range(1, PAIRS):
+            load_h(pair)
         load_weight("wq", wq)
         load_weight("wv", wv)
 
         ident = kept([P, P], F32, "ident")
         make_identity(nc, ident[:])
 
+        grouped = {side: kept([P, PACK * B], BF16, side + "_grouped") for side in ("h", "q", "p")}
         mx = {}
 
-        def quantize(name, lo=0, hi=None):
-            src = grouped[name]
-            width = src.shape[1] // PACK
+        def quantize(name, half=None):
+            width = grouped[name].shape[1] // PACK
             if name not in mx:
                 mx[name] = (kept([P, width], U32, name + "_codes"), kept([P, width], U8, name + "_scales"))
-            hi = width if hi is None else hi
+            lo, hi = (0, width) if half is None else (half * width // 2, (half + 1) * width // 2)
             codes, scales = mx[name]
             nc.vector.quantize_mx(
-                out=codes[:, lo:hi].bitcast(FP8X4), scales=scales[:, lo:hi], in_=src[:, PACK * lo : PACK * hi]
+                out=codes[:, lo:hi].bitcast(FP8X4),
+                scales=scales[:, lo:hi],
+                in_=grouped[name][:, PACK * lo : PACK * hi],
             )
 
         def matmul(dst, stationary, s_cols, moving, m_cols):
@@ -115,57 +106,65 @@ def tile_aitmadaptiveinformationtransfer_kernel(tc, h_prev, q_bytes, q_scale, wg
                 stop=True,
             )
 
-        def w_grouped(name, slot):
+        def copy_on_gpsimd(dst, src):
+            nc.gpsimd.tensor_scalar(out=dst, in0=src, scalar1=1.0, scalar2=0.0, op0=ALU.mult, op1=ALU.add)
+
+        def copy_on_scalar(dst, src):
+            nc.scalar.activation(out=dst, in_=src, func=ACT.Copy)
+
+        def new_grouped_weight(name, slot):
             grouped[name] = keep.tile([P, PACK * D], BF16, name=name + "_grouped", tag=slot, align_bytes=256)
 
-        def interleave(name, engine, lo, hi):
+        def regroup(name, copy, lo, hi):
             dst = grouped[name][:, PACK * lo : PACK * hi].rearrange("p (c i j) -> p c j i", i=RUN, j=PACK)
             src = raw[name][:].rearrange("p (j c) -> p j c", j=PACK)[:, :, lo:hi]
-            copy_on(engine, dst, src.rearrange("p j (c i) -> p c j i", i=RUN))
+            copy(dst, src.rearrange("p j (c i) -> p c j i", i=RUN))
 
-        def interleave_wg(engine, lo, hi):
+        def regroup_shared(name):
+            regroup(name, copy_on_gpsimd, 0, GPSIMD_COLUMNS[name])
+            regroup(name, copy_on_scalar, GPSIMD_COLUMNS[name], D)
+
+        def regroup_wg(copy, lo, hi):
             dst = grouped["wg"][:].rearrange("p (t m j) -> p m t j", t=PACK, j=PACK)[:, :, lo:hi]
             src = raw["wg"][:].rearrange("p (j m t) -> p m t j", j=PACK, t=PACK)[:, :, lo:hi]
-            copy_on(engine, dst, src)
+            copy(dst, src)
 
-        scale_bank = psum.tile([P, D], F32, name="scale_bank", tag="b7")
-        for t in range(PACK):
-            nc.tensor.transpose(scale_bank[:, t::PACK], scale_cols[:, t : t + 1].to_broadcast([P, P]), ident[:])
+        def spread_scale(bank):
+            spread = bank_tile(bank)
+            for t in range(PACK):
+                nc.tensor.transpose(spread[:, t::PACK], scale_cols[:, t : t + 1].to_broadcast([P, P]), ident[:])
+            return spread
 
-        q_sb = {}
-
-        def widen_q(i):
-            pair, half = divmod(i, 2)
-            if half == 0:
-                q_sb[pair] = kept([P, 2 * D], BF16, "q_sb%d" % pair)
+        def widen_q(i, spread):
+            pair, side_of_pair = divmod(i, 2)
+            if side_of_pair == 0:
+                rows["q", pair] = kept([P, 2 * D], BF16, "q_rows%d" % pair)
             nc.vector.tensor_tensor(
-                out=q_sb[pair][:, D * half : D * (half + 1)],
-                in0=q_in[i // PAIRS][:, D * (i % PAIRS) : D * (i % PAIRS + 1)].bitcast(FP8),
-                in1=scale_bank[:],
+                out=rows["q", pair][:, D * side_of_pair : D * (side_of_pair + 1)],
+                in0=q_in[i // HALF][:, D * (i % HALF) : D * (i % HALF + 1)].bitcast(FP8),
+                in1=spread[:],
                 op=ALU.mult,
             )
 
-        for side in ("h", "q", "p"):
-            grouped[side] = keep.tile([P, PACK * B], BF16, name=side + "_grouped", tag="slot_" + side, align_bytes=256)
-        turn_bank = {}
+        turned = {}
 
-        def turn(side, pair, tag):
-            words = (h_sb if side == "h" else q_sb)[pair][:].bitcast(F32)
-            turn_bank[side, pair] = psum.tile([P, D], F32, name="turn_bank", tag=tag)
-            for half in range(2):
+        def turn(side, pair, bank):
+            words = rows[side, pair][:].bitcast(F32)
+            turned[side, pair] = bank_tile(bank)
+            for tile in range(2):
                 for u in range(2):
-                    col = P * (2 * half + u)
+                    col = P * (2 * tile + u)
                     nc.tensor.transpose(
-                        turn_bank[side, pair][:, col : col + P],
-                        words[:, 2 * P * half + u : 2 * P * (half + 1) : 2],
+                        turned[side, pair][:, col : col + P],
+                        words[:, 2 * P * tile + u : 2 * P * (tile + 1) : 2],
                         ident[:],
                     )
 
-        def empty_turn(side, pair):
+        def empty_turned(side, pair):
             dst = grouped[side][:, 2 * D * pair : 2 * D * (pair + 1)].bitcast(F32)
             nc.scalar.copy(
                 out=dst.rearrange("p (i n u) -> p i n u", i=2, u=2),
-                in_=turn_bank[side, pair][:].rearrange("p (i u n) -> p i n u", i=2, u=2),
+                in_=turned[side, pair][:].rearrange("p (i u n) -> p i n u", i=2, u=2),
             )
 
         def tokens(i):
@@ -173,207 +172,199 @@ def tile_aitmadaptiveinformationtransfer_kernel(tc, h_prev, q_bytes, q_scale, wg
 
         p_bank = {}
 
-        def project_p(i, tag):
-            p_bank[i] = psum.tile([P, D], F32, name="p_bank", tag=tag)
+        def project_p(i, bank):
+            p_bank[i] = bank_tile(bank)
             for t in range(PACK):
                 cols = slice(P * t, P * (t + 1))
                 matmul(p_bank[i][:, cols], "wg", cols, "h", tokens(i))
 
         def add_bias(i):
             nc.vector.tensor_tensor(
-                out=grouped["p"][:, D * i : D * (i + 1)].rearrange("p (n i t) -> p n t i", i=2, t=PACK),
-                in0=p_bank[i][:].rearrange("p (t n i) -> p n t i", i=2, t=PACK),
+                out=grouped["p"][:, D * i : D * (i + 1)].rearrange("p (n e t) -> p n t e", e=2, t=PACK),
+                in0=p_bank[i][:].rearrange("p (t n e) -> p n t e", e=2, t=PACK),
                 in1=bias_cols[:].unsqueeze(1).unsqueeze(3).to_broadcast([P, P // 2, PACK, 2]),
                 op=ALU.add,
             )
 
-        everything = slice(0, D)
         key_sb = {}
         query_bank = {}
+        value_bank = {}
         score = {}
+        gate = {}
+        z_sb = {}
+        col_p, col_q, col_tanh = slice(0, 1), slice(1, 2), slice(2, 3)
 
-        key_bank = {}
+        def project(side, i, weight, bank):
+            result = bank_tile(bank)
+            matmul(result[:], side, tokens(i), weight, slice(0, D))
+            return result
 
-        def project(side, i, weight, bank, tag):
-            bank[side, i] = psum.tile([P, D], F32, name="result_bank", tag=tag)
-            matmul(bank[side, i][:], side, tokens(i), weight, everything)
-
-        def copy_key(side, i):
+        def key(side, i, bank):
+            result = project(side, i, "wk", bank)
             key_sb[side, i] = kept([P, D], F32, "key_%s%d" % (side, i))
-            nc.scalar.copy(out=key_sb[side, i][:], in_=key_bank[side, i][:])
+            nc.scalar.copy(out=key_sb[side, i][:], in_=result[:])
+
+        def query(side, i):
+            query_bank[side, i] = project(side, i, "wq", {"q": (4, 6), "p": (5, 7)}[side][i % 2])
+
+        def values(i):
+            ring = (3, 1, 0)
+            banks = {LAST - 2: (1, 2), LAST - 1: (0, 4), LAST: (1, 5)}.get(i, (ring[2 * i % 3], ring[(2 * i + 1) % 3]))
+            value_bank["p", i] = project("p", i, "wv", banks[0])
+            value_bank["q", i] = project("q", i, "wv", banks[1])
 
         def scores(side, i):
             score[side, i] = kept([P, 1], F32, "score_%s%d" % (side, i))
+            factor = 0.5 / math.sqrt(D)
             nc.vector.scalar_tensor_tensor(
                 out=key_sb[side, i][:],
                 in0=query_bank[side, i][:],
-                scalar=half_inv_sqrt if side == "p" else -half_inv_sqrt,
+                scalar=factor if side == "p" else -factor,
                 in1=key_sb[side, i][:],
                 op0=ALU.mult,
                 op1=ALU.mult,
                 accum_out=score[side, i][:],
             )
 
-        gate = {}
-        value_bank = {}
-        z_sb = {}
-
-        def gates(i):
+        def gate_tanh(i):
             gate[i] = kept([P, 3], F32, "gate%d" % i)
-            nc.scalar.activation(out=gate[i][:, 2:3], in_=score["p", i][:], func=ACT.Tanh, bias=score["q", i][:])
+            nc.scalar.activation(out=gate[i][:, col_tanh], in_=score["p", i][:], func=ACT.Tanh, bias=score["q", i][:])
 
-        def gates2(i):
-            for col, sign in ((0, 0.5), (1, -0.5)):
+        def gate_weights(i):
+            for col, sign in ((col_p, 0.5), (col_q, -0.5)):
                 nc.scalar.activation(
-                    out=gate[i][:, col : col + 1], in_=gate[i][:, 2:3], func=ACT.Identity, scale=sign, bias=0.5
+                    out=gate[i][:, col], in_=gate[i][:, col_tanh], func=ACT.Identity, scale=sign, bias=0.5
                 )
 
         def weigh_p(i, lo=0, hi=D):
             if lo == 0:
                 z_sb[i] = work.tile([P, D], F32, name="z_sb", tag="z_sb")
             nc.scalar.activation(
-                out=z_sb[i][:, lo:hi], in_=value_bank["p", i][:, lo:hi], func=ACT.Copy, scale=gate[i][:, 0:1]
+                out=z_sb[i][:, lo:hi], in_=value_bank["p", i][:, lo:hi], func=ACT.Copy, scale=gate[i][:, col_p]
             )
 
-        def combine(i, lo=0, hi=D):
+        def store(i, lo=0, hi=D):
+            nc.sync.dma_start(out=out_rows[:, D * i + lo : D * i + hi], in_=z_sb[i][:, lo:hi])
+
+        def sum_on_vector(i, lo=0, hi=D):
             nc.vector.scalar_tensor_tensor(
                 out=z_sb[i][:, lo:hi],
                 in0=value_bank["q", i][:, lo:hi],
-                scalar=gate[i][:, 1:2],
+                scalar=gate[i][:, col_q],
                 in1=z_sb[i][:, lo:hi],
                 op0=ALU.mult,
                 op1=ALU.add,
             )
-            nc.sync.dma_start(out=out_rows[:, D * i + lo : D * i + hi], in_=z_sb[i][:, lo:hi])
+            store(i, lo, hi)
 
-        def combine_aside(i):
+        def sum_aside(i):
             zq_sb = work.tile([P, D], F32, name="zq_sb", tag="zq_sb")
-            nc.scalar.activation(out=zq_sb[:], in_=value_bank["q", i][:], func=ACT.Copy, scale=gate[i][:, 1:2])
+            nc.scalar.activation(out=zq_sb[:], in_=value_bank["q", i][:], func=ACT.Copy, scale=gate[i][:, col_q])
             nc.gpsimd.tensor_tensor(out=z_sb[i][:], in0=z_sb[i][:], in1=zq_sb[:], op=ALU.add)
 
-        def store(i):
-            nc.sync.dma_start(out=out_rows[:, D * i : D * (i + 1)], in_=z_sb[i][:])
+        spread = spread_scale(7)
+        new_grouped_weight("wg", "slot_wg")
+        new_grouped_weight("wk", "slot_shared")
+        regroup_wg(copy_on_gpsimd, 0, PACK // 2)
+        regroup_wg(copy_on_scalar, PACK // 2, PACK)
+        regroup_shared("wk")
+        for pair in range(2):
+            widen_q(2 * pair, spread)
+            widen_q(2 * pair + 1, spread)
+            turn("q", pair, pair)
+        empty_turned("q", 0)
+        turn("h", 0, 2)
+        turn("h", 1, 3)
+        empty_turned("h", 0)
+        empty_turned("h", 1)
+        empty_turned("q", 1)
+        for i in range(HALF, TILES):
+            widen_q(i, spread)
+        turn("q", 2, 0)
+        turn("h", 2, 4)
+        turn("h", 3, 5)
+        turn("q", 3, 2)
+        for side in ("h", "q"):
+            empty_turned(side, 2)
+            empty_turned(side, 3)
 
-        w_grouped("wg", "slot_a")
-        w_grouped("wk", "slot_b")
-        w_grouped("wq", "slot_c")
-        interleave_wg("gpsimd", 0, WG_V)
-        interleave_wg("scalar", WG_V, 4)
-        interleave("wk", "gpsimd", 0, WK_V)
-        widen_q(0)
-        widen_q(1)
-        turn("q", 0, "b0")
-        empty_turn("q", 0)
-        if WK_V < D:
-            interleave("wk", "scalar", WK_V, D)
-        widen_q(2)
-        widen_q(3)
-        turn("q", 1, "b1")
-        turn("h", 0, "b2")
-        turn("h", 1, "b3")
-        empty_turn("h", 0)
-        empty_turn("h", 1)
-        empty_turn("q", 1)
-        for i in range(4, TILES):
-            widen_q(i)
-        turn("q", 2, "b0")
-        turn("h", 2, "b4")
-        turn("h", 3, "b5")
-        turn("q", 3, "b2")
-        empty_turn("h", 2)
-        empty_turn("h", 3)
-        empty_turn("q", 2)
-        empty_turn("q", 3)
-        half = B // 2
-        last = TILES - 1
-        p_tags = ("b6", "b7", "b3", "b4", "b5")
-        key_tags = ("b0", "b1", "b2")
-        v_tags = ("b3", "b0", "b1")
-
-        def key(side, i, tag):
-            project(side, i, "wk", key_bank, tag)
-            copy_key(side, i)
-
-        def queries(i):
-            project("q", i, "wq", query_bank, ("b4", "b6")[i % 2])
-            project("p", i, "wq", query_bank, ("b5", "b7")[i % 2])
-
-        interleave("wq", "scalar", 0, D)
+        p_banks = (6, 7, 3, 4, 5)
         quantize("wg")
-        quantize("h", 0, half)
-        for i in range(4):
-            project_p(i, p_tags[i])
+        quantize("h", 0)
+        for i in range(HALF):
+            project_p(i, p_banks[i])
+        quantize("q", 0)
         quantize("wk")
-        quantize("q", 0, half)
-        add_bias(0)
-        quantize("h", half, B)
-        add_bias(1)
-        for i in range(4, 7):
-            project_p(i, p_tags[i % 5])
-        for i in range(3):
-            key("q", i, key_tags[i])
-        quantize("q", half, B)
-        add_bias(2)
-        project_p(7, p_tags[2])
-        key("q", 3, key_tags[0])
-        add_bias(3)
-        add_bias(4)
-        quantize("p", 0, half)
-        quantize("wq")
-        w_grouped("wv", "slot_c")
-        interleave("wv", "gpsimd", 0, D)
-        for i in range(5, TILES):
+
+        new_grouped_weight("wq", "slot_shared")
+        regroup_shared("wq")
+        for i in range(HALF):
+            key("q", i, i % 3)
+        for i in range(HALF):
             add_bias(i)
-        early = [("p", 0), ("q", 4), ("p", 1), ("q", 5), ("p", 2), ("q", 6), ("p", 3), ("q", 7)]
-        for n, (side, i) in enumerate(early):
-            key(side, i, key_tags[(n + 1) % 3])
-            if n in (1, 3):
-                queries(n // 2)
-            if n == 5:
-                scores("q", 0)
-                scores("p", 0)
-                queries(2)
-                gates(0)
-        gates2(0)
+        quantize("q", 1)
+        quantize("h", 1)
+        for i in (HALF, HALF + 1):
+            key("q", i, i % 3)
+        for i in (HALF, HALF + 1):
+            project_p(i, p_banks[i % 5])
+        quantize("p", 0)
+        key("p", 0, 0)
+        for i in (HALF + 2, HALF + 3):
+            project_p(i, p_banks[i % 5])
+        key("p", 1, 1)
+        quantize("wq")
 
-        value_tags = {last - 1: ("b2", v_tags[1]), last: ("b4", "b5")}
+        new_grouped_weight("wv", "slot_shared")
+        regroup_shared("wv")
+        for i in range(HALF, TILES):
+            add_bias(i)
+        key("q", LAST - 1, 2)
+        query("q", 0)
+        query("p", 0)
+        key("p", 2, 0)
+        key("q", LAST, 1)
+        query("q", 1)
+        key("p", 3, 2)
+        query("p", 1)
+        scores("q", 0)
+        quantize("p", 1)
+        scores("p", 0)
+        quantize("wv")
+        key("p", 4, 0)
+        query("q", 2)
+        gate_tanh(0)
+        key("p", 5, 2)
+        gate_weights(0)
+        values(0)
+        query("p", 2)
 
-        def values(i):
-            tags = value_tags.get(i, (v_tags[(2 * i) % 3], v_tags[(2 * i + 1) % 3]))
-            project("p", i, "wv", value_bank, tags[0])
-            return tags[1]
-
-        for s in range(1, TILES + 1):
-            if s < TILES:
-                scores("q", s)
-                scores("p", s)
+        for s in range(1, TILES):
+            scores("q", s)
+            scores("p", s)
             if s + 2 < TILES:
-                queries(s + 2)
-            if s == 1:
-                quantize("wv")
-                quantize("p", half, B)
-                project("q", 0, "wv", value_bank, values(0))
-            if s == last:
+                query("q", s + 2)
+            if s == LAST:
                 weigh_p(s - 1)
-            if s < TILES:
-                gates(s)
-            if s < last:
+            gate_tanh(s)
+            if s < LAST:
                 weigh_p(s - 1)
-            if s < TILES:
-                gates2(s)
+            gate_weights(s)
             if s - 1 in ASIDE:
-                combine_aside(s - 1)
-            if 2 <= s and s - 2 not in ASIDE:
-                combine(s - 2)
+                sum_aside(s - 1)
             if s - 2 in ASIDE:
                 store(s - 2)
-            if s < TILES:
-                tag = values(s)
-            if s + 3 < TILES:
-                key("p", s + 3, "b2")
-            if s < TILES:
-                project("q", s, "wv", value_bank, tag)
+            elif 2 <= s < LAST - 1:
+                sum_on_vector(s - 2)
+            if s + 2 < TILES:
+                query("p", s + 2)
+            if s + 5 < TILES:
+                key("p", s + 5, 2)
+            values(s)
+
+        for i in range(LAST - 3, LAST):
+            sum_on_vector(i)
         for lo in (0, D // 2):
-            weigh_p(TILES - 1, lo, lo + D // 2)
+            weigh_p(LAST, lo, lo + D // 2)
         for lo in (0, D // 2):
-            combine(TILES - 1, lo, lo + D // 2)
+            sum_on_vector(LAST, lo, lo + D // 2)

import math
from contextlib import ExitStack

import concourse.mybir as mybir
from concourse.masks import make_identity

B, D = 1024, 512
FLOPS = 7 * 2 * B * D * D

F32 = mybir.dt.float32
BF16 = mybir.dt.bfloat16
U32 = mybir.dt.uint32
U8 = mybir.dt.uint8
FP8 = mybir.dt.float8_e4m3fn
FP8X4 = mybir.dt.float8_e4m3fn_x4
ALU = mybir.AluOpType
ACT = mybir.ActivationFunctionType

P = 128
PACK = 4
TILES = B // P
PAIRS = TILES // 2
HALF = TILES // 2
LAST = TILES - 1
RUN = 4

GPSIMD_COLUMNS = {"wk": 256, "wq": 320, "wv": 384}
ASIDE = (1, 2, 3)
Z_BUFS = 5


def tile_aitmadaptiveinformationtransfer_kernel(tc, h_prev, q_bytes, q_scale, wg, bg, wv, wk, wq, out):
    nc = tc.nc
    h_rows = h_prev.rearrange("(p i) k -> p (i k)", i=TILES)
    q_rows = q_bytes.rearrange("(p i) k -> p (i k)", i=TILES)
    out_rows = out.rearrange("(p i) k -> p (i k)", i=TILES)

    with ExitStack() as ctx:
        keep = ctx.enter_context(tc.tile_pool(name="keep", bufs=1))
        work = ctx.enter_context(tc.tile_pool(name="work", bufs=Z_BUFS))
        psum = ctx.enter_context(tc.psum_pool(name="psum", bufs=1))
        ctx.enter_context(tc.manual_schedule())

        def kept(shape, dtype, name):
            return keep.tile(shape, dtype, name=name, align_bytes=256)

        def bank_tile(bank):
            return psum.tile([P, D], F32, name="bank", tag="bank%d" % bank)

        raw = {}
        rows = {}
        q_in = {}

        def load_weight(name, w):
            raw[name] = kept([P, PACK * D], BF16, name + "_raw")
            nc.sync.dma_start(out=raw[name][:], in_=w.rearrange("(p j) c -> p (j c)", j=PACK))

        def load_h(pair):
            rows["h", pair] = kept([P, 2 * D], BF16, "h_rows%d" % pair)
            nc.sync.dma_start(out=rows["h", pair][:], in_=h_rows[:, 2 * D * pair : 2 * D * (pair + 1)])

        def load_q(half):
            q_in[half] = kept([P, HALF * D], U8, "q_bytes_sb%d" % half)
            nc.sync.dma_start(out=q_in[half][:], in_=q_rows[:, HALF * D * half : HALF * D * (half + 1)])

        scale_cols = kept([P, PACK], F32, "scale_cols")
        nc.sync.dma_start(out=scale_cols[:], in_=q_scale.rearrange("o (p t) -> p (o t)", t=PACK))
        load_q(0)
        load_weight("wg", wg)
        load_weight("wk", wk)
        load_q(1)
        load_h(0)
        bias_cols = kept([P, PACK], BF16, "bias_cols")
        nc.sync.dma_start(out=bias_cols[:], in_=bg.rearrange("(p t) -> p t", t=PACK))
        for pair in range(1, PAIRS):
            load_h(pair)
        load_weight("wq", wq)
        load_weight("wv", wv)

        ident = kept([P, P], F32, "ident")
        make_identity(nc, ident[:])

        grouped = {side: kept([P, PACK * B], BF16, side + "_grouped") for side in ("h", "q", "p")}
        mx = {}

        def quantize(name, half=None):
            width = grouped[name].shape[1] // PACK
            if name not in mx:
                mx[name] = (kept([P, width], U32, name + "_codes"), kept([P, width], U8, name + "_scales"))
            lo, hi = (0, width) if half is None else (half * width // 2, (half + 1) * width // 2)
            codes, scales = mx[name]
            nc.vector.quantize_mx(
                out=codes[:, lo:hi].bitcast(FP8X4),
                scales=scales[:, lo:hi],
                in_=grouped[name][:, PACK * lo : PACK * hi],
            )

        def matmul(dst, stationary, s_cols, moving, m_cols):
            nc.tensor.matmul_mx(
                out=dst,
                lhsT=mx[stationary][0][:, s_cols].bitcast(FP8X4),
                lhsT_scale=mx[stationary][1][:, s_cols],
                rhs=mx[moving][0][:, m_cols].bitcast(FP8X4),
                rhs_scale=mx[moving][1][:, m_cols],
                start=True,
                stop=True,
            )

        def copy_on_gpsimd(dst, src):
            nc.gpsimd.tensor_scalar(out=dst, in0=src, scalar1=1.0, scalar2=0.0, op0=ALU.mult, op1=ALU.add)

        def copy_on_scalar(dst, src):
            nc.scalar.activation(out=dst, in_=src, func=ACT.Copy)

        def new_grouped_weight(name, slot):
            grouped[name] = keep.tile([P, PACK * D], BF16, name=name + "_grouped", tag=slot, align_bytes=256)

        def regroup(name, copy, lo, hi):
            dst = grouped[name][:, PACK * lo : PACK * hi].rearrange("p (c i j) -> p c j i", i=RUN, j=PACK)
            src = raw[name][:].rearrange("p (j c) -> p j c", j=PACK)[:, :, lo:hi]
            copy(dst, src.rearrange("p j (c i) -> p c j i", i=RUN))

        def regroup_shared(name):
            regroup(name, copy_on_gpsimd, 0, GPSIMD_COLUMNS[name])
            regroup(name, copy_on_scalar, GPSIMD_COLUMNS[name], D)

        def regroup_wg(copy, lo, hi):
            dst = grouped["wg"][:].rearrange("p (t m j) -> p m t j", t=PACK, j=PACK)[:, :, lo:hi]
            src = raw["wg"][:].rearrange("p (j m t) -> p m t j", j=PACK, t=PACK)[:, :, lo:hi]
            copy(dst, src)

        def spread_scale(bank):
            spread = bank_tile(bank)
            for t in range(PACK):
                nc.tensor.transpose(spread[:, t::PACK], scale_cols[:, t : t + 1].to_broadcast([P, P]), ident[:])
            return spread

        def widen_q(i, spread):
            pair, side_of_pair = divmod(i, 2)
            if side_of_pair == 0:
                rows["q", pair] = kept([P, 2 * D], BF16, "q_rows%d" % pair)
            nc.vector.tensor_tensor(
                out=rows["q", pair][:, D * side_of_pair : D * (side_of_pair + 1)],
                in0=q_in[i // HALF][:, D * (i % HALF) : D * (i % HALF + 1)].bitcast(FP8),
                in1=spread[:],
                op=ALU.mult,
            )

        turned = {}

        def turn(side, pair, bank):
            words = rows[side, pair][:].bitcast(F32)
            turned[side, pair] = bank_tile(bank)
            for tile in range(2):
                for u in range(2):
                    col = P * (2 * tile + u)
                    nc.tensor.transpose(
                        turned[side, pair][:, col : col + P],
                        words[:, 2 * P * tile + u : 2 * P * (tile + 1) : 2],
                        ident[:],
                    )

        def empty_turned(side, pair):
            dst = grouped[side][:, 2 * D * pair : 2 * D * (pair + 1)].bitcast(F32)
            nc.scalar.copy(
                out=dst.rearrange("p (i n u) -> p i n u", i=2, u=2),
                in_=turned[side, pair][:].rearrange("p (i u n) -> p i n u", i=2, u=2),
            )

        def tokens(i):
            return slice(P * i, P * (i + 1))

        p_bank = {}

        def project_p(i, bank):
            p_bank[i] = bank_tile(bank)
            for t in range(PACK):
                cols = slice(P * t, P * (t + 1))
                matmul(p_bank[i][:, cols], "wg", cols, "h", tokens(i))

        def add_bias(i):
            nc.vector.tensor_tensor(
                out=grouped["p"][:, D * i : D * (i + 1)].rearrange("p (n e t) -> p n t e", e=2, t=PACK),
                in0=p_bank[i][:].rearrange("p (t n e) -> p n t e", e=2, t=PACK),
                in1=bias_cols[:].unsqueeze(1).unsqueeze(3).to_broadcast([P, P // 2, PACK, 2]),
                op=ALU.add,
            )

        key_sb = {}
        query_bank = {}
        value_bank = {}
        score = {}
        gate = {}
        z_sb = {}
        col_p, col_q, col_tanh = slice(0, 1), slice(1, 2), slice(2, 3)

        def project(side, i, weight, bank):
            result = bank_tile(bank)
            matmul(result[:], side, tokens(i), weight, slice(0, D))
            return result

        def key(side, i, bank):
            result = project(side, i, "wk", bank)
            key_sb[side, i] = kept([P, D], F32, "key_%s%d" % (side, i))
            nc.scalar.copy(out=key_sb[side, i][:], in_=result[:])

        def query(side, i):
            query_bank[side, i] = project(side, i, "wq", {"q": (4, 6), "p": (5, 7)}[side][i % 2])

        def values(i):
            ring = (3, 1, 0)
            banks = {LAST - 2: (1, 2), LAST - 1: (0, 4), LAST: (1, 5)}.get(i, (ring[2 * i % 3], ring[(2 * i + 1) % 3]))
            value_bank["p", i] = project("p", i, "wv", banks[0])
            value_bank["q", i] = project("q", i, "wv", banks[1])

        def scores(side, i):
            score[side, i] = kept([P, 1], F32, "score_%s%d" % (side, i))
            factor = 0.5 / math.sqrt(D)
            nc.vector.scalar_tensor_tensor(
                out=key_sb[side, i][:],
                in0=query_bank[side, i][:],
                scalar=factor if side == "p" else -factor,
                in1=key_sb[side, i][:],
                op0=ALU.mult,
                op1=ALU.mult,
                accum_out=score[side, i][:],
            )

        def gate_tanh(i):
            gate[i] = kept([P, 3], F32, "gate%d" % i)
            nc.scalar.activation(out=gate[i][:, col_tanh], in_=score["p", i][:], func=ACT.Tanh, bias=score["q", i][:])

        def gate_weights(i):
            for col, sign in ((col_p, 0.5), (col_q, -0.5)):
                nc.scalar.activation(
                    out=gate[i][:, col], in_=gate[i][:, col_tanh], func=ACT.Identity, scale=sign, bias=0.5
                )

        def weigh_p(i, lo=0, hi=D):
            if lo == 0:
                z_sb[i] = work.tile([P, D], F32, name="z_sb", tag="z_sb")
            nc.scalar.activation(
                out=z_sb[i][:, lo:hi], in_=value_bank["p", i][:, lo:hi], func=ACT.Copy, scale=gate[i][:, col_p]
            )

        def store(i, lo=0, hi=D):
            nc.sync.dma_start(out=out_rows[:, D * i + lo : D * i + hi], in_=z_sb[i][:, lo:hi])

        def sum_on_vector(i, lo=0, hi=D):
            nc.vector.scalar_tensor_tensor(
                out=z_sb[i][:, lo:hi],
                in0=value_bank["q", i][:, lo:hi],
                scalar=gate[i][:, col_q],
                in1=z_sb[i][:, lo:hi],
                op0=ALU.mult,
                op1=ALU.add,
            )
            store(i, lo, hi)

        def sum_aside(i):
            zq_sb = work.tile([P, D], F32, name="zq_sb", tag="zq_sb")
            nc.scalar.activation(out=zq_sb[:], in_=value_bank["q", i][:], func=ACT.Copy, scale=gate[i][:, col_q])
            nc.gpsimd.tensor_tensor(out=z_sb[i][:], in0=z_sb[i][:], in1=zq_sb[:], op=ALU.add)

        spread = spread_scale(7)
        new_grouped_weight("wg", "slot_wg")
        new_grouped_weight("wk", "slot_shared")
        regroup_wg(copy_on_gpsimd, 0, PACK // 2)
        regroup_wg(copy_on_scalar, PACK // 2, PACK)
        regroup_shared("wk")
        for pair in range(2):
            widen_q(2 * pair, spread)
            widen_q(2 * pair + 1, spread)
            turn("q", pair, pair)
        empty_turned("q", 0)
        turn("h", 0, 2)
        turn("h", 1, 3)
        empty_turned("h", 0)
        empty_turned("h", 1)
        empty_turned("q", 1)
        for i in range(HALF, TILES):
            widen_q(i, spread)
        turn("q", 2, 0)
        turn("h", 2, 4)
        turn("h", 3, 5)
        turn("q", 3, 2)
        for side in ("h", "q"):
            empty_turned(side, 2)
            empty_turned(side, 3)

        p_banks = (6, 7, 3, 4, 5)
        quantize("wg")
        quantize("h", 0)
        for i in range(HALF):
            project_p(i, p_banks[i])
        quantize("q", 0)
        quantize("wk")

        new_grouped_weight("wq", "slot_shared")
        regroup_shared("wq")
        for i in range(HALF):
            key("q", i, i % 3)
        for i in range(HALF):
            add_bias(i)
        quantize("q", 1)
        quantize("h", 1)
        for i in (HALF, HALF + 1):
            key("q", i, i % 3)
        for i in (HALF, HALF + 1):
            project_p(i, p_banks[i % 5])
        quantize("p", 0)
        key("p", 0, 0)
        for i in (HALF + 2, HALF + 3):
            project_p(i, p_banks[i % 5])
        key("p", 1, 1)
        quantize("wq")

        new_grouped_weight("wv", "slot_shared")
        regroup_shared("wv")
        for i in range(HALF, TILES):
            add_bias(i)
        key("q", LAST - 1, 2)
        query("q", 0)
        query("p", 0)
        key("p", 2, 0)
        key("q", LAST, 1)
        query("q", 1)
        key("p", 3, 2)
        query("p", 1)
        scores("q", 0)
        quantize("p", 1)
        scores("p", 0)
        quantize("wv")
        key("p", 4, 0)
        query("q", 2)
        gate_tanh(0)
        key("p", 5, 2)
        gate_weights(0)
        values(0)
        query("p", 2)

        for s in range(1, TILES):
            scores("q", s)
            scores("p", s)
            if s + 2 < TILES:
                query("q", s + 2)
            if s == LAST:
                weigh_p(s - 1)
            gate_tanh(s)
            if s < LAST:
                weigh_p(s - 1)
            gate_weights(s)
            if s - 1 in ASIDE:
                sum_aside(s - 1)
            if s - 2 in ASIDE:
                store(s - 2)
            elif 2 <= s < LAST - 1:
                sum_on_vector(s - 2)
            if s + 2 < TILES:
                query("p", s + 2)
            if s + 5 < TILES:
                key("p", s + 5, 2)
            values(s)

        for i in range(LAST - 3, LAST):
            sum_on_vector(i)
        for lo in (0, D // 2):
            weigh_p(LAST, lo, lo + D // 2)
        for lo in (0, D // 2):
            sum_on_vector(LAST, lo, lo + D // 2)
